import numpy as np
import ml_dtypes


def mxq(x, axis, fmt="e4m3"):
    dtype, down = {"e4m3": (ml_dtypes.float8_e4m3fn, 7), "e5m2": (ml_dtypes.float8_e5m2, 14)}[fmt]
    v = np.moveaxis(np.asarray(x, np.float32).astype(ml_dtypes.bfloat16).astype(np.float64), axis, -1)
    blocks = v.reshape(v.shape[:-1] + (-1, 32))
    amax = np.abs(blocks).max(-1, keepdims=True)
    byte = np.maximum(np.where(amax > 0, np.frexp(amax)[1] - 1 + 127, 0) - down, 1)
    scale = np.exp2(byte - 127.0)
    codes = (blocks / scale).astype(np.float32).astype(dtype).astype(np.float64)
    return np.moveaxis((codes * scale).reshape(v.shape), -1, axis)


WIDE = False


def mx_kscale(k):
    if not WIDE:
        return np.ones(k)
    levels = np.array([10, -10, 5, -5, 0])
    if k % 512:
        return np.exp2(np.random.permutation(np.resize(levels, k // 32))).repeat(32)
    a = np.empty((k // 512, 16))
    for p in range(k // 512):
        a[p, :8] = np.random.permutation(np.resize(levels, 8))
        for g in range(8):
            far = levels[np.abs(levels - a[p, g]) >= 10]
            a[p, g + 8] = far[np.random.randint(len(far))]
    return np.exp2(a.ravel()).repeat(32)


BF16 = ml_dtypes.bfloat16


def bf(x):
    return np.asarray(x, np.float32).astype(BF16)


def f64(x):
    return np.asarray(x).astype(np.float64)


N, Q, R = 1024, 1024, 512


def draw0():
    t = mx_kscale(Q)
    u = mx_kscale(R)
    r = mx_kscale(N)
    return {
        "x1": bf(np.random.standard_normal((N, Q))),
        "x2": bf(np.random.standard_normal((N, R))),
        "w1": bf(np.random.standard_normal((Q, R)) / np.sqrt(Q) / t[:, None]),
        "v1": bf(np.random.standard_normal((R, Q)) / np.sqrt(R) / u[:, None]),
        "g": bf((1.0 + 0.1 * np.random.standard_normal(Q)) * t),
        "pi2": bf(np.random.uniform(0.5, 1.5, R) * u),
        "a": bf((1.0 + 0.1 * np.random.standard_normal(N)) * r),
        "c": bf((1.0 + 0.1 * np.random.standard_normal(N)) / r),
    }


def core(x1, x2, w1, v1, g, pi2, a, c):
    x1, x2, w1, v1 = f64(x1), f64(x2), f64(w1), f64(v1)
    g, pi2, a, c = f64(g), f64(pi2), f64(a), f64(c)
    n = x1.shape[0]
    f = np.tanh(x1)
    mu = mxq(f * g[None, :], 1, "e4m3") @ mxq(w1, 0, "e4m3")
    eps = x2 - mu
    back = mxq(eps * pi2[None, :], 1, "e4m3") @ mxq(v1, 0, "e4m3")
    x1_new = x1 + 0.5 * (-x1 + (1.0 - f * f) * back)
    dw1 = (mxq(f * a[:, None], 0, "e4m3").T @ mxq(eps * c[:, None], 0, "e4m3")) / np.sqrt(n)
    return x1_new, dw1


def e4m3fn_bytes(y):
    return np.clip(np.asarray(y, np.float64), -448.0, 448.0).astype(np.float32).astype(ml_dtypes.float8_e4m3fn).view(np.uint8)


def e4m3fn_values(b):
    return np.asarray(b, np.uint8).view(ml_dtypes.float8_e4m3fn).astype(np.float64)


def setup_inputs():
    d = draw0()
    x0 = np.asarray(d['w1']).astype(np.float64)
    s = (np.max(np.abs(x0), axis=(1,), keepdims=True) / 448.0).astype(np.float32)
    out = {}
    for k, v in d.items():
        if k == 'w1':
            out['w1_bytes'] = e4m3fn_bytes(x0 / s.astype(np.float64))
            out['w1_scale'] = s
        else:
            out[k] = v
    return out


def reference(x1, x2, w1_bytes, w1_scale, v1, g, pi2, a, c):
    return core(x1, x2, e4m3fn_values(w1_bytes) * w1_scale.astype(np.float64), v1, g, pi2, a, c)

@@ -1,0 +1,305 @@
+from contextlib import ExitStack
+
+import concourse.mybir as mybir
+from concourse.masks import make_identity
+
+N, Q, R = 1024, 1024, 512
+P = 128
+FLOPS = 3 * 2 * N * Q * R
+
+F32 = mybir.dt.float32
+BF16 = mybir.dt.bfloat16
+U32 = mybir.dt.uint32
+U8 = mybir.dt.uint8
+FP8 = mybir.dt.float8_e4m3fn
+FP8X4 = mybir.dt.float8_e4m3fn_x4
+ALU = mybir.AluOpType
+ACT = mybir.ActivationFunctionType
+
+HALF_ROOT = 0.5 ** 0.5
+
+
+def tile_incrementalpredictivecodingupdate_kernel(tc, x1, x2, w1_bytes, w1_scale, v1, g, pi2, a, c, out_0, out_1):
+    nc = tc.nc
+    x1v = x1.rearrange("(g p t) q -> g p t q", p=P, t=4)
+    x2v = x2.rearrange("(g p t) r -> g p t r", p=P, t=4)
+    w1v = w1_bytes.rearrange("(g p t) r -> g p t r", p=P, t=4)
+    v1v = v1.rearrange("(p t) q -> p t q", t=4)
+    xov = out_0.rearrange("(g p t) q -> g p t q", p=P, t=4)
+
+    with ExitStack() as ctx:
+        keep = ctx.enter_context(tc.tile_pool(name="keep", bufs=1))
+        work = ctx.enter_context(tc.tile_pool(name="work", bufs=2))
+        psum = ctx.enter_context(tc.psum_pool(name="psum", bufs=1))
+
+        x1s = keep.tile([P, 2, 4, Q], BF16, name="x1s")
+        x2s = keep.tile([P, 2, 4, R], BF16, name="x2s")
+        w1b = keep.tile([P, 2, 4, R], U8, name="w1b")
+        w1s = keep.tile([P, 2, 4], F32, name="w1s")
+        v1s = keep.tile([P, 4, Q], BF16, name="v1s")
+        gs = keep.tile([P, 2, 4], BF16, name="gs")
+        as_ = keep.tile([P, 2, 4], BF16, name="as_")
+        cs = keep.tile([P, 2, 4], BF16, name="cs")
+        ps = keep.tile([P, 4], BF16, name="ps")
+        ident = keep.tile([P, P], F32, name="ident")
+
+        f = keep.tile([P, 2, 4, Q], F32, name="f")
+        eps = keep.tile([P, 2, 4, R], F32, name="eps")
+        w1p = keep.tile([P, 2, 4, R], BF16, name="w1p")
+        w1i = keep.tile([P, 2, R, 4], BF16, name="w1i", align_bytes=64)
+        v1i = keep.tile([P, Q, 4], BF16, name="v1i", align_bytes=64)
+        fap = keep.tile([P, 2, 4, Q], BF16, name="fap")
+        fai = keep.tile([P, 2, Q, 4], BF16, name="fai", align_bytes=64)
+        w1c = keep.tile([P, 2 * R], U32, name="w1c", align_bytes=64)
+        w1e = keep.tile([P, 2 * R], U8, name="w1e", align_bytes=64)
+        v1c = keep.tile([P, Q], U32, name="v1c", align_bytes=64)
+        v1e = keep.tile([P, Q], U8, name="v1e", align_bytes=64)
+        fac = keep.tile([P, 2 * Q], U32, name="fac", align_bytes=64)
+        fae = keep.tile([P, 2 * Q], U8, name="fae", align_bytes=64)
+        ecc = keep.tile([P, 2 * R], U32, name="ecc", align_bytes=64)
+        ece = keep.tile([P, 2 * R], U8, name="ece", align_bytes=64)
+
+        with tc.manual_schedule():
+            nc.scalar.dma_start(out=w1s[:], in_=w1_scale.rearrange("(g p t) o -> p g (t o)", p=P, t=4))
+            nc.sync.dma_start(out=w1b[:, 0], in_=w1v[0])
+            nc.sync.dma_start(out=x1s[:, 0, 0, :], in_=x1v[0][:, 0, :])
+            nc.sync.dma_start(out=w1b[:, 1], in_=w1v[1])
+            for t in (1, 2, 3):
+                nc.sync.dma_start(out=x1s[:, 0, t, :], in_=x1v[0][:, t, :])
+            nc.sync.dma_start(out=x2s[:, 0], in_=x2v[0])
+            for h in (0, 1):
+                nc.sync.dma_start(out=v1s[:, :, h * 512:(h + 1) * 512], in_=v1v[:, :, h * 512:(h + 1) * 512])
+            for t in (0, 2):
+                nc.sync.dma_start(out=x1s[:, 1, t:t + 2, :], in_=x1v[1][:, t:t + 2, :])
+            nc.sync.dma_start(out=x2s[:, 1], in_=x2v[1])
+            nc.gpsimd.dma_start(out=gs[:], in_=g.rearrange("(g p t) -> p g t", p=P, t=4))
+            make_identity(nc, ident[:])
+            nc.gpsimd.dma_start(out=as_[:], in_=a.rearrange("(g p t) -> p g t", p=P, t=4))
+            nc.gpsimd.dma_start(out=ps[:], in_=pi2.rearrange("(p t) -> p t", t=4))
+            nc.gpsimd.dma_start(out=cs[:], in_=c.rearrange("(g p t) -> p g t", p=P, t=4))
+
+            warm = keep.tile([P, 1], F32, name="warm")
+            warm2 = keep.tile([P, 1], F32, name="warm2")
+            nc.vector.memset(warm[:], 0.0)
+            nc.scalar.activation(out=warm2[:], in_=warm[:], func=ACT.Tanh)
+
+            af = keep.tile([P, 2, 4], F32, name="af")
+            nc.gpsimd.tensor_copy(out=af[:], in_=as_[:])
+
+            def tanh(i):
+                nc.scalar.activation(out=f[:, i // 4, i % 4, :], in_=x1s[:, i // 4, i % 4, :], func=ACT.Tanh)
+
+            hs = {}
+
+            def square(i):
+                h = work.tile([P, Q], F32, name="h", bufs=3)
+                nc.scalar.activation(out=h[:], in_=f[:, i // 4, i % 4, :], func=ACT.Square, scale=HALF_ROOT)
+                hs[i] = h
+
+            fts = {}
+
+            def trans_f(i):
+                for k in (0, 1):
+                    ft = psum.tile([P, 4, P], F32, name="ft", tag="ft", bufs=4)
+                    for t in range(4):
+                        nc.tensor.transpose(ft[:, t, :], f[:, i // 4, i % 4, k * 512 + t:(k + 1) * 512:4], ident[:])
+                    fts[i, k] = ft
+
+            fgs = {}
+
+            def mul_g(i):
+                fg = work.tile([P, 2, P, 4], BF16, name="fg", align_bytes=64)
+                for k in (0, 1):
+                    nc.vector.tensor_tensor(out=fg[:, k], in0=fts[i, k][:].rearrange("p t n -> p n t"),
+                                            in1=gs[:, k, :].unsqueeze(1).to_broadcast([P, P, 4]), op=ALU.mult)
+                fgs[i] = fg
+
+            fgq = {}
+
+            def quant_fg(i):
+                cd = work.tile([P, 2 * P], U32, name="fgc", align_bytes=64)
+                sc = work.tile([P, 2 * P], U8, name="fge", align_bytes=64)
+                nc.vector.quantize_mx(out=cd[:].bitcast(FP8X4), scales=sc[:], in_=fgs[i][:].rearrange("p k n t -> p (k n t)"))
+                fgq[i] = (cd, sc)
+
+            mus = {}
+
+            def mm1(i):
+                mu = psum.tile([P, R], F32, name="mu", tag="mu")
+                cd, sc = fgq[i]
+                for k in (0, 1):
+                    nc.tensor.matmul_mx(out=mu[:], lhsT=cd[:, k * P:(k + 1) * P].bitcast(FP8X4), lhsT_scale=sc[:, k * P:(k + 1) * P],
+                                        rhs=w1c[:, k * R:(k + 1) * R].bitcast(FP8X4), rhs_scale=w1e[:, k * R:(k + 1) * R],
+                                        start=(k == 0), stop=(k == 1))
+                mus[i] = mu
+
+            def error(i):
+                nc.vector.tensor_tensor(out=eps[:, i // 4, i % 4, :], in0=x2s[:, i // 4, i % 4, :], in1=mus[i][:], op=ALU.subtract)
+
+            ets = {}
+
+            def trans_e(i):
+                et = psum.tile([P, 4, P], F32, name="et", tag="et")
+                for t in range(4):
+                    nc.tensor.transpose(et[:, t, :], eps[:, i // 4, i % 4, t::4], ident[:])
+                ets[i] = et
+
+            eps_ = {}
+
+            def mul_p(i):
+                ep = work.tile([P, P, 4], BF16, name="ep", align_bytes=64)
+                nc.vector.tensor_tensor(out=ep[:], in0=ets[i][:].rearrange("p t n -> p n t"),
+                                        in1=ps[:].unsqueeze(1).to_broadcast([P, P, 4]), op=ALU.mult)
+                eps_[i] = ep
+
+            epq = {}
+
+            def quant_ep(i):
+                cd = work.tile([P, P], U32, name="epc", align_bytes=64)
+                sc = work.tile([P, P], U8, name="epe", align_bytes=64)
+                nc.vector.quantize_mx(out=cd[:].bitcast(FP8X4), scales=sc[:], in_=eps_[i][:].rearrange("p n t -> p (n t)"))
+                epq[i] = (cd, sc)
+
+            bks = {}
+
+            def mm2(i):
+                cd, sc = epq[i]
+                for h in (0, 1):
+                    bk = psum.tile([P, 512], F32, name="bk", tag="bk", bufs=2)
+                    nc.tensor.matmul_mx(out=bk[:], lhsT=cd[:].bitcast(FP8X4), lhsT_scale=sc[:],
+                                        rhs=v1c[:, h * 512:(h + 1) * 512].bitcast(FP8X4), rhs_scale=v1e[:, h * 512:(h + 1) * 512],
+                                        start=True, stop=True)
+                    bks[i, h] = bk
+
+            us = {}
+
+            def delta(i):
+                u = work.tile([P, Q], F32, name="u")
+                for h in (0, 1):
+                    s = slice(h * 512, (h + 1) * 512)
+                    nc.vector.scalar_tensor_tensor(out=u[:, s], in0=hs[i][:, s], scalar=0.5, in1=bks[i, h][:], op0=ALU.subtract, op1=ALU.mult)
+                us[i] = u
+
+            def state(i):
+                o = work.tile([P, Q], F32, name="o", bufs=3)
+                nc.vector.scalar_tensor_tensor(out=o[:], in0=x1s[:, i // 4, i % 4, :], scalar=0.5, in1=us[i][:], op0=ALU.mult, op1=ALU.subtract)
+                nc.sync.dma_start(out=xov[i // 4][:, i % 4, :], in_=o[:])
+
+            def scale_fa(i):
+                nc.scalar.activation(out=fap[:, i // 4, i % 4, :], in_=f[:, i // 4, i % 4, :], func=ACT.Copy, scale=af[:, i // 4, i % 4:i % 4 + 1])
+
+            def inter(eng_copy, out, in_):
+                eng_copy(out=out.rearrange("p (c i) t -> p c t i", i=4), in_=in_.rearrange("p t (c i) -> p c t i", i=4))
+
+            def inter_fa(k, h):
+                inter(nc.scalar.copy, fai[:, k, h * 256:(h + 1) * 256, :], fap[:, k, :, h * 256:(h + 1) * 256])
+
+            def quant_fa(k, h):
+                o = k * Q + h * 512
+                nc.vector.quantize_mx(out=fac[:, o:o + 512].bitcast(FP8X4), scales=fae[:, o:o + 512],
+                                      in_=fai[:, k, h * 512:(h + 1) * 512, :].rearrange("p q t -> p (q t)"))
+
+            ecs = {}
+
+            def mul_c(k, h):
+                if h == 0:
+                    ec = work.tile([P, R, 4], BF16, name="ec", align_bytes=64)
+                    ecs[k] = ec
+                s = slice(h * 256, (h + 1) * 256)
+                nc.vector.tensor_tensor(out=ecs[k][:, s, :].rearrange("p (c i) t -> p c t i", i=4),
+                                        in0=eps[:, k, :, s].rearrange("p t (c i) -> p c t i", i=4),
+                                        in1=cs[:, k, :].unsqueeze(1).unsqueeze(3).to_broadcast([P, 64, 4, 4]), op=ALU.mult)
+
+            def quant_ec(k):
+                nc.vector.quantize_mx(out=ecc[:, k * R:(k + 1) * R].bitcast(FP8X4), scales=ece[:, k * R:(k + 1) * R],
+                                      in_=ecs[k][:].rearrange("p r t -> p (r t)"))
+
+            def mm3(m):
+                dw = psum.tile([P, R], F32, name="dw", tag="ft", bufs=4)
+                for k in (0, 1):
+                    o = k * Q + m * P
+                    nc.tensor.matmul_mx(out=dw[:], lhsT=fac[:, o:o + P].bitcast(FP8X4), lhsT_scale=fae[:, o:o + P],
+                                        rhs=ecc[:, k * R:(k + 1) * R].bitcast(FP8X4), rhs_scale=ece[:, k * R:(k + 1) * R],
+                                        start=(k == 0), stop=(k == 1))
+                d = work.tile([P, R], F32, name="d", bufs=4)
+                nc.scalar.activation(out=d[:], in_=dw[:], func=ACT.Copy, scale=0.03125)
+                nc.sync.dma_start(out=out_1[m * P:(m + 1) * P, :], in_=d[:])
+
+            def widen(k, t):
+                nc.vector.tensor_scalar(out=w1p[:, k, t, :], in0=w1b[:, k, t, :].bitcast(FP8), scalar1=w1s[:, k, t:t + 1], scalar2=None, op0=ALU.mult)
+
+            def quant_w1(k):
+                nc.vector.quantize_mx(out=w1c[:, k * R:(k + 1) * R].bitcast(FP8X4), scales=w1e[:, k * R:(k + 1) * R],
+                                      in_=w1i[:, k].rearrange("p r t -> p (r t)"))
+
+            def inter_v1(h):
+                inter(nc.scalar.copy, v1i[:, h * 256:(h + 1) * 256, :], v1s[:, :, h * 256:(h + 1) * 256])
+
+            def quant_v1(h):
+                nc.vector.quantize_mx(out=v1c[:, h * 512:(h + 1) * 512].bitcast(FP8X4), scales=v1e[:, h * 512:(h + 1) * 512],
+                                      in_=v1i[:, h * 512:(h + 1) * 512, :].rearrange("p q t -> p (q t)"))
+
+            for i in range(4):
+                tanh(i)
+            for k in (0, 1):
+                for t in range(4):
+                    widen(k, t)
+            trans_f(0)
+            for k in (0, 1):
+                inter(nc.vector.tensor_copy, w1i[:, k], w1p[:, k])
+            for k in (0, 1):
+                quant_w1(k)
+
+            for s in range(10):
+                if s < 4:
+                    tanh(s + 4)
+                    if s < 2:
+                        inter_v1(2 * s)
+                        inter_v1(2 * s + 1)
+                if 1 <= s <= 8:
+                    error(s - 1)
+                    trans_e(s - 1)
+                if s < 8:
+                    mul_g(s)
+                    if s < 7:
+                        trans_f(s + 1)
+                if 1 <= s <= 4:
+                    scale_fa(2 * s - 2)
+                    scale_fa(2 * s - 1)
+                if s == 4:
+                    mul_c(0, 0)
+                if s == 5:
+                    mul_c(0, 1)
+                if s == 8:
+                    mul_c(1, 0)
+                    mul_c(1, 1)
+                if 1 <= s <= 8:
+                    mul_p(s - 1)
+                if s < 8:
+                    quant_fg(s)
+                    mm1(s)
+                if s == 1:
+                    quant_v1(0)
+                    quant_v1(1)
+                if s == 6:
+                    quant_ec(0)
+                if s == 8:
+                    quant_ec(1)
+                if 2 <= s <= 9:
+                    delta(s - 2)
+                if 1 <= s <= 8:
+                    quant_ep(s - 1)
+                    mm2(s - 1)
+                    square(s - 1)
+                if 3 <= s <= 6:
+                    k = (s - 3) // 2
+                    h = (s - 3) % 2
+                    inter_fa(k, 2 * h)
+                    inter_fa(k, 2 * h + 1)
+                if 5 <= s <= 8:
+                    quant_fa((s - 5) // 2, (s - 5) % 2)
+                if 2 <= s <= 9:
+                    state(s - 2)
+                if s == 8:
+                    for m in range(8):
+                        mm3(m)

@@ -17,6 +17,7 @@ ALU = mybir.AluOpType
 ACT = mybir.ActivationFunctionType
 
 HALF_ROOT = 0.5 ** 0.5
+ON_G = (0, 1, 2, 3, 4)
 
 
 def tile_incrementalpredictivecodingupdate_kernel(tc, x1, x2, w1_bytes, w1_scale, v1, g, pi2, a, c, out_0, out_1):
@@ -46,10 +47,15 @@ def tile_incrementalpredictivecodingupdate_kernel(tc, x1, x2, w1_bytes, w1_scale
         f = keep.tile([P, 2, 4, Q], F32, name="f")
         eps = keep.tile([P, 2, 4, R], F32, name="eps")
         w1p = keep.tile([P, 2, 4, R], BF16, name="w1p")
-        w1i = keep.tile([P, 2, R, 4], BF16, name="w1i", align_bytes=64)
-        v1i = keep.tile([P, Q, 4], BF16, name="v1i", align_bytes=64)
-        fap = keep.tile([P, 2, 4, Q], BF16, name="fap")
-        fai = keep.tile([P, 2, Q, 4], BF16, name="fai", align_bytes=64)
+        w1i = keep.tile([P, 2, R, 4], BF16, name="w1i", tag="inter", bufs=3, align_bytes=64)
+        v1i = keep.tile([P, Q, 4], BF16, name="v1i", tag="inter", bufs=3, align_bytes=64)
+        fai = []
+        fap = []
+        for k in (0, 1):
+            fai_k = keep.tile([P, Q, 4], BF16, name="fai%d" % k, tag="inter", bufs=3, align_bytes=64)
+            fai.append(fai_k)
+            fap_k = keep.tile([P, 4, Q], BF16, name="fap%d" % k)
+            fap.append(fap_k)
         w1c = keep.tile([P, 2 * R], U32, name="w1c", align_bytes=64)
         w1e = keep.tile([P, 2 * R], U8, name="w1e", align_bytes=64)
         v1c = keep.tile([P, Q], U32, name="v1c", align_bytes=64)
@@ -61,19 +67,21 @@ def tile_incrementalpredictivecodingupdate_kernel(tc, x1, x2, w1_bytes, w1_scale
 
         with tc.manual_schedule():
             nc.scalar.dma_start(out=w1s[:], in_=w1_scale.rearrange("(g p t) o -> p g (t o)", p=P, t=4))
+            nc.scalar.dma_start(out=gs[:], in_=g.rearrange("(g p t) -> p g t", p=P, t=4))
             nc.sync.dma_start(out=w1b[:, 0], in_=w1v[0])
             nc.sync.dma_start(out=x1s[:, 0, 0, :], in_=x1v[0][:, 0, :])
             nc.sync.dma_start(out=w1b[:, 1], in_=w1v[1])
             for t in (1, 2, 3):
                 nc.sync.dma_start(out=x1s[:, 0, t, :], in_=x1v[0][:, t, :])
+            nc.sync.dma_start(out=v1s[:, :, 0:512], in_=v1v[:, :, 0:512])
             nc.sync.dma_start(out=x2s[:, 0], in_=x2v[0])
-            for h in (0, 1):
-                nc.sync.dma_start(out=v1s[:, :, h * 512:(h + 1) * 512], in_=v1v[:, :, h * 512:(h + 1) * 512])
+            nc.sync.dma_start(out=v1s[:, :, 512:1024], in_=v1v[:, :, 512:1024])
             for t in (0, 2):
                 nc.sync.dma_start(out=x1s[:, 1, t:t + 2, :], in_=x1v[1][:, t:t + 2, :])
             nc.sync.dma_start(out=x2s[:, 1], in_=x2v[1])
-            nc.gpsimd.dma_start(out=gs[:], in_=g.rearrange("(g p t) -> p g t", p=P, t=4))
             make_identity(nc, ident[:])
+            identb = keep.tile([P, P], BF16, name="identb")
+            nc.gpsimd.tensor_copy(out=identb[:], in_=ident[:])
             nc.gpsimd.dma_start(out=as_[:], in_=a.rearrange("(g p t) -> p g t", p=P, t=4))
             nc.gpsimd.dma_start(out=ps[:], in_=pi2.rearrange("(p t) -> p t", t=4))
             nc.gpsimd.dma_start(out=cs[:], in_=c.rearrange("(g p t) -> p g t", p=P, t=4))
@@ -172,6 +180,13 @@ def tile_incrementalpredictivecodingupdate_kernel(tc, x1, x2, w1_bytes, w1_scale
                     bks[i, h] = bk
 
             us = {}
+            xh = {}
+
+            def half_x(i):
+                if i in ON_G:
+                    y = work.tile([P, Q], BF16, name="y", bufs=3)
+                    nc.vector.tensor_scalar(out=y[:], in0=x1s[:, i // 4, i % 4, :], scalar1=0.5, scalar2=None, op0=ALU.mult)
+                    xh[i] = y
 
             def delta(i):
                 u = work.tile([P, Q], F32, name="u")
@@ -182,22 +197,29 @@ def tile_incrementalpredictivecodingupdate_kernel(tc, x1, x2, w1_bytes, w1_scale
 
             def state(i):
                 o = work.tile([P, Q], F32, name="o", bufs=3)
-                nc.vector.scalar_tensor_tensor(out=o[:], in0=x1s[:, i // 4, i % 4, :], scalar=0.5, in1=us[i][:], op0=ALU.mult, op1=ALU.subtract)
+                if i in ON_G:
+                    nc.gpsimd.tensor_tensor(out=o[:], in0=xh[i][:], in1=us[i][:], op=ALU.subtract)
+                else:
+                    nc.vector.scalar_tensor_tensor(out=o[:], in0=x1s[:, i // 4, i % 4, :], scalar=0.5, in1=us[i][:], op0=ALU.mult, op1=ALU.subtract)
                 nc.sync.dma_start(out=xov[i // 4][:, i % 4, :], in_=o[:])
 
             def scale_fa(i):
-                nc.scalar.activation(out=fap[:, i // 4, i % 4, :], in_=f[:, i // 4, i % 4, :], func=ACT.Copy, scale=af[:, i // 4, i % 4:i % 4 + 1])
+                nc.scalar.activation(out=fap[i // 4][:, i % 4, :], in_=f[:, i // 4, i % 4, :], func=ACT.Copy, scale=af[:, i // 4, i % 4:i % 4 + 1])
 
             def inter(eng_copy, out, in_):
                 eng_copy(out=out.rearrange("p (c i) t -> p c t i", i=4), in_=in_.rearrange("p t (c i) -> p c t i", i=4))
 
             def inter_fa(k, h):
-                inter(nc.scalar.copy, fai[:, k, h * 256:(h + 1) * 256, :], fap[:, k, :, h * 256:(h + 1) * 256])
+                pk = psum.tile([P, 256, 4], BF16, name="pk", tag="ft", bufs=4)
+                for e in (0, 1):
+                    q0 = h * 256 + e * P
+                    nc.tensor.matmul(pk[:, e * P:(e + 1) * P, :], lhsT=identb[:], rhs=fap[k][:, :, q0:q0 + P].rearrange("p t q -> p q t"), start=True, stop=True)
+                nc.scalar.copy(out=fai[k][:, h * 256:(h + 1) * 256, :], in_=pk[:])
 
             def quant_fa(k, h):
                 o = k * Q + h * 512
                 nc.vector.quantize_mx(out=fac[:, o:o + 512].bitcast(FP8X4), scales=fae[:, o:o + 512],
-                                      in_=fai[:, k, h * 512:(h + 1) * 512, :].rearrange("p q t -> p (q t)"))
+                                      in_=fai[k][:, h * 512:(h + 1) * 512, :].rearrange("p q t -> p (q t)"))
 
             ecs = {}
 
@@ -221,7 +243,7 @@ def tile_incrementalpredictivecodingupdate_kernel(tc, x1, x2, w1_bytes, w1_scale
                     nc.tensor.matmul_mx(out=dw[:], lhsT=fac[:, o:o + P].bitcast(FP8X4), lhsT_scale=fae[:, o:o + P],
                                         rhs=ecc[:, k * R:(k + 1) * R].bitcast(FP8X4), rhs_scale=ece[:, k * R:(k + 1) * R],
                                         start=(k == 0), stop=(k == 1))
-                d = work.tile([P, R], F32, name="d", bufs=4)
+                d = work.tile([P, R], F32, name="d", bufs=8)
                 nc.scalar.activation(out=d[:], in_=dw[:], func=ACT.Copy, scale=0.03125)
                 nc.sync.dma_start(out=out_1[m * P:(m + 1) * P, :], in_=d[:])
 
@@ -239,67 +261,96 @@ def tile_incrementalpredictivecodingupdate_kernel(tc, x1, x2, w1_bytes, w1_scale
                 nc.vector.quantize_mx(out=v1c[:, h * 512:(h + 1) * 512].bitcast(FP8X4), scales=v1e[:, h * 512:(h + 1) * 512],
                                       in_=v1i[:, h * 512:(h + 1) * 512, :].rearrange("p q t -> p (q t)"))
 
-            for i in range(4):
+            LEAD = 3
+            for i in range(2):
                 tanh(i)
             for k in (0, 1):
                 for t in range(4):
                     widen(k, t)
             trans_f(0)
-            for k in (0, 1):
-                inter(nc.vector.tensor_copy, w1i[:, k], w1p[:, k])
-            for k in (0, 1):
-                quant_w1(k)
+            inter(nc.vector.tensor_copy, w1i[:, 0], w1p[:, 0])
+            inter(nc.scalar.copy, w1i[:, 1, :256], w1p[:, 1, :, :256])
+            quant_w1(0)
+            inter(nc.vector.tensor_copy, w1i[:, 1, 256:], w1p[:, 1, :, 256:])
+            tanh(2)
+            tanh(3)
+            inter_v1(0)
+            inter_v1(1)
+            inter_v1(2)
+            inter_v1(3)
+            for i in range(4, 8):
+                tanh(i)
+            side = [(scale_fa, i) for i in range(8)]
+            nside = 0
 
-            for s in range(10):
-                if s < 4:
-                    tanh(s + 4)
-                    if s < 2:
-                        inter_v1(2 * s)
-                        inter_v1(2 * s + 1)
-                if 1 <= s <= 8:
+            for s in range(8):
+                j = s - 2
+                mul_g(s)
+                if s < 7:
+                    trans_f(s + 1)
+                if s == 0:
+                    quant_w1(1)
+                if s >= 1:
                     error(s - 1)
-                    trans_e(s - 1)
-                if s < 8:
-                    mul_g(s)
-                    if s < 7:
-                        trans_f(s + 1)
-                if 1 <= s <= 4:
-                    scale_fa(2 * s - 2)
-                    scale_fa(2 * s - 1)
+                if j >= 0:
+                    mul_p(j)
+                if s == 2:
+                    half_x(0)
+                quant_fg(s)
+                mm1(s)
+                if s == 2:
+                    quant_v1(0)
+                    quant_v1(1)
+                if j >= 0:
+                    quant_ep(j)
+                    mm2(j)
+                if j + 1 >= 0:
+                    trans_e(j + 1)
+                for k, h in {5: ((0, 0), (0, 1)), 6: ((0, 2), (0, 3)), 7: ((1, 0), (1, 1), (1, 2), (1, 3))}.get(s, ()):
+                    inter_fa(k, h)
                 if s == 4:
                     mul_c(0, 0)
                 if s == 5:
                     mul_c(0, 1)
-                if s == 8:
-                    mul_c(1, 0)
-                    mul_c(1, 1)
-                if 1 <= s <= 8:
-                    mul_p(s - 1)
-                if s < 8:
-                    quant_fg(s)
-                    mm1(s)
-                if s == 1:
-                    quant_v1(0)
-                    quant_v1(1)
                 if s == 6:
                     quant_ec(0)
-                if s == 8:
-                    quant_ec(1)
-                if 2 <= s <= 9:
-                    delta(s - 2)
-                if 1 <= s <= 8:
-                    quant_ep(s - 1)
-                    mm2(s - 1)
-                    square(s - 1)
-                if 3 <= s <= 6:
-                    k = (s - 3) // 2
-                    h = (s - 3) % 2
-                    inter_fa(k, 2 * h)
-                    inter_fa(k, 2 * h + 1)
-                if 5 <= s <= 8:
-                    quant_fa((s - 5) // 2, (s - 5) % 2)
-                if 2 <= s <= 9:
-                    state(s - 2)
-                if s == 8:
-                    for m in range(8):
-                        mm3(m)
+                    quant_fa(0, 0)
+                if s == 7:
+                    quant_fa(0, 1)
+                if j >= 0:
+                    half_x(j + 1)
+                if 0 <= j < 5:
+                    square(j)
+                while nside < (0, 0, 0, 3, 6, 8, 8, 8)[s]:
+                    side[nside][0](*side[nside][1:])
+                    nside += 1
+                if j >= 1:
+                    delta(j - 1)
+                    state(j - 1)
+
+            error(7)
+            mul_p(6)
+            trans_e(7)
+            quant_ep(6)
+            mm2(6)
+            mul_c(1, 0)
+            mul_p(7)
+            mul_c(1, 1)
+            quant_ep(7)
+            quant_fa(1, 0)
+            quant_fa(1, 1)
+            quant_ec(1)
+            square(5)
+            square(6)
+            for m in range(6):
+                mm3(m)
+            delta(5)
+            state(5)
+            delta(6)
+            mm2(7)
+            square(7)
+            for m in range(6, 8):
+                mm3(m)
+            state(6)
+            delta(7)
+            state(7)

@@ -80,8 +80,6 @@ def tile_incrementalpredictivecodingupdate_kernel(tc, x1, x2, w1_bytes, w1_scale
                 nc.sync.dma_start(out=x1s[:, 1, t:t + 2, :], in_=x1v[1][:, t:t + 2, :])
             nc.sync.dma_start(out=x2s[:, 1], in_=x2v[1])
             make_identity(nc, ident[:])
-            identb = keep.tile([P, P], BF16, name="identb")
-            nc.gpsimd.tensor_copy(out=identb[:], in_=ident[:])
             nc.gpsimd.dma_start(out=as_[:], in_=a.rearrange("(g p t) -> p g t", p=P, t=4))
             nc.gpsimd.dma_start(out=ps[:], in_=pi2.rearrange("(p t) -> p t", t=4))
             nc.gpsimd.dma_start(out=cs[:], in_=c.rearrange("(g p t) -> p g t", p=P, t=4))
@@ -210,11 +208,7 @@ def tile_incrementalpredictivecodingupdate_kernel(tc, x1, x2, w1_bytes, w1_scale
                 eng_copy(out=out.rearrange("p (c i) t -> p c t i", i=4), in_=in_.rearrange("p t (c i) -> p c t i", i=4))
 
             def inter_fa(k, h):
-                pk = psum.tile([P, 256, 4], BF16, name="pk", tag="ft", bufs=4)
-                for e in (0, 1):
-                    q0 = h * 256 + e * P
-                    nc.tensor.matmul(pk[:, e * P:(e + 1) * P, :], lhsT=identb[:], rhs=fap[k][:, :, q0:q0 + P].rearrange("p t q -> p q t"), start=True, stop=True)
-                nc.scalar.copy(out=fai[k][:, h * 256:(h + 1) * 256, :], in_=pk[:])
+                inter(nc.scalar.copy, fai[k][:, h * 256:(h + 1) * 256, :], fap[k][:, :, h * 256:(h + 1) * 256])
 
             def quant_fa(k, h):
                 o = k * Q + h * 512
@@ -262,6 +256,7 @@ def tile_incrementalpredictivecodingupdate_kernel(tc, x1, x2, w1_bytes, w1_scale
                                       in_=v1i[:, h * 512:(h + 1) * 512, :].rearrange("p q t -> p (q t)"))
 
             LEAD = 3
+            SIDE = (0, 0, 0, 3, 6, 9, 12, 16)
             for i in range(2):
                 tanh(i)
             for k in (0, 1):
@@ -280,7 +275,9 @@ def tile_incrementalpredictivecodingupdate_kernel(tc, x1, x2, w1_bytes, w1_scale
             inter_v1(3)
             for i in range(4, 8):
                 tanh(i)
-            side = [(scale_fa, i) for i in range(8)]
+            side = []
+            for k in (0, 1):
+                side += [(scale_fa, 4 * k + t) for t in range(4)] + [(inter_fa, k, h) for h in range(4)]
             nside = 0
 
             for s in range(8):
@@ -306,8 +303,6 @@ def tile_incrementalpredictivecodingupdate_kernel(tc, x1, x2, w1_bytes, w1_scale
                     mm2(j)
                 if j + 1 >= 0:
                     trans_e(j + 1)
-                for k, h in {5: ((0, 0), (0, 1)), 6: ((0, 2), (0, 3)), 7: ((1, 0), (1, 1), (1, 2), (1, 3))}.get(s, ()):
-                    inter_fa(k, h)
                 if s == 4:
                     mul_c(0, 0)
                 if s == 5:
@@ -321,7 +316,7 @@ def tile_incrementalpredictivecodingupdate_kernel(tc, x1, x2, w1_bytes, w1_scale
                     half_x(j + 1)
                 if 0 <= j < 5:
                     square(j)
-                while nside < (0, 0, 0, 3, 6, 8, 8, 8)[s]:
+                while nside < SIDE[s]:
                     side[nside][0](*side[nside][1:])
                     nside += 1
                 if j >= 1:

@@ -17,7 +17,7 @@ ALU = mybir.AluOpType
 ACT = mybir.ActivationFunctionType
 
 HALF_ROOT = 0.5 ** 0.5
-ON_G = (0, 1, 2, 3, 4)
+ON_G = (0, 1, 2, 3)
 
 
 def tile_incrementalpredictivecodingupdate_kernel(tc, x1, x2, w1_bytes, w1_scale, v1, g, pi2, a, c, out_0, out_1):
@@ -26,6 +26,7 @@ def tile_incrementalpredictivecodingupdate_kernel(tc, x1, x2, w1_bytes, w1_scale
     x2v = x2.rearrange("(g p t) r -> g p t r", p=P, t=4)
     w1v = w1_bytes.rearrange("(g p t) r -> g p t r", p=P, t=4)
     v1v = v1.rearrange("(p t) q -> p t q", t=4)
+    dwv = out_1.rearrange("(k p u) r -> k u p r", k=2, u=4)
     xov = out_0.rearrange("(g p t) q -> g p t q", p=P, t=4)
 
     with ExitStack() as ctx:
@@ -70,6 +71,7 @@ def tile_incrementalpredictivecodingupdate_kernel(tc, x1, x2, w1_bytes, w1_scale
             nc.scalar.dma_start(out=gs[:], in_=g.rearrange("(g p t) -> p g t", p=P, t=4))
             nc.sync.dma_start(out=w1b[:, 0], in_=w1v[0])
             nc.sync.dma_start(out=x1s[:, 0, 0, :], in_=x1v[0][:, 0, :])
+            nc.scalar.dma_start(out=as_[:], in_=a.rearrange("(g p t) -> p g t", p=P, t=4))
             nc.sync.dma_start(out=w1b[:, 1], in_=w1v[1])
             for t in (1, 2, 3):
                 nc.sync.dma_start(out=x1s[:, 0, t, :], in_=x1v[0][:, t, :])
@@ -80,7 +82,6 @@ def tile_incrementalpredictivecodingupdate_kernel(tc, x1, x2, w1_bytes, w1_scale
                 nc.sync.dma_start(out=x1s[:, 1, t:t + 2, :], in_=x1v[1][:, t:t + 2, :])
             nc.sync.dma_start(out=x2s[:, 1], in_=x2v[1])
             make_identity(nc, ident[:])
-            nc.gpsimd.dma_start(out=as_[:], in_=a.rearrange("(g p t) -> p g t", p=P, t=4))
             nc.gpsimd.dma_start(out=ps[:], in_=pi2.rearrange("(p t) -> p t", t=4))
             nc.gpsimd.dma_start(out=cs[:], in_=c.rearrange("(g p t) -> p g t", p=P, t=4))
 
@@ -93,13 +94,17 @@ def tile_incrementalpredictivecodingupdate_kernel(tc, x1, x2, w1_bytes, w1_scale
             nc.gpsimd.tensor_copy(out=af[:], in_=as_[:])
 
             def tanh(i):
-                nc.scalar.activation(out=f[:, i // 4, i % 4, :], in_=x1s[:, i // 4, i % 4, :], func=ACT.Tanh)
+                nc.scalar.activation(out=f[:, i // 4, i % 4, :].rearrange("p (k u m) -> p k u m", k=2, u=4),
+                                     in_=x1s[:, i // 4, i % 4, :].rearrange("p (k m u) -> p k u m", k=2, u=4), func=ACT.Tanh)
 
             hs = {}
 
             def square(i):
                 h = work.tile([P, Q], F32, name="h", bufs=3)
-                nc.scalar.activation(out=h[:], in_=f[:, i // 4, i % 4, :], func=ACT.Square, scale=HALF_ROOT)
+                for k in (0, 1):
+                    s = slice(k * 512, (k + 1) * 512)
+                    nc.scalar.activation(out=h[:, s].rearrange("p (b j u) -> p b u j", j=4, u=4),
+                                         in_=f[:, i // 4, i % 4, s].rearrange("p (u b j) -> p b u j", u=4, j=4), func=ACT.Square, scale=HALF_ROOT)
                 hs[i] = h
 
             fts = {}
@@ -108,7 +113,7 @@ def tile_incrementalpredictivecodingupdate_kernel(tc, x1, x2, w1_bytes, w1_scale
                 for k in (0, 1):
                     ft = psum.tile([P, 4, P], F32, name="ft", tag="ft", bufs=4)
                     for t in range(4):
-                        nc.tensor.transpose(ft[:, t, :], f[:, i // 4, i % 4, k * 512 + t:(k + 1) * 512:4], ident[:])
+                        nc.tensor.transpose(ft[:, t, :], f[:, i // 4, i % 4, k * 512 + t * P:k * 512 + (t + 1) * P], ident[:])
                     fts[i, k] = ft
 
             fgs = {}
@@ -140,14 +145,16 @@ def tile_incrementalpredictivecodingupdate_kernel(tc, x1, x2, w1_bytes, w1_scale
                 mus[i] = mu
 
             def error(i):
-                nc.vector.tensor_tensor(out=eps[:, i // 4, i % 4, :], in0=x2s[:, i // 4, i % 4, :], in1=mus[i][:], op=ALU.subtract)
+                nc.vector.tensor_tensor(out=eps[:, i // 4, i % 4, :].rearrange("p (u m) -> p u m", u=4),
+                                        in0=x2s[:, i // 4, i % 4, :].rearrange("p (m u) -> p u m", u=4),
+                                        in1=mus[i][:].rearrange("p (m u) -> p u m", u=4), op=ALU.subtract)
 
             ets = {}
 
             def trans_e(i):
                 et = psum.tile([P, 4, P], F32, name="et", tag="et")
                 for t in range(4):
-                    nc.tensor.transpose(et[:, t, :], eps[:, i // 4, i % 4, t::4], ident[:])
+                    nc.tensor.transpose(et[:, t, :], eps[:, i // 4, i % 4, t * P:(t + 1) * P], ident[:])
                 ets[i] = et
 
             eps_ = {}
@@ -187,7 +194,7 @@ def tile_incrementalpredictivecodingupdate_kernel(tc, x1, x2, w1_bytes, w1_scale
                     xh[i] = y
 
             def delta(i):
-                u = work.tile([P, Q], F32, name="u")
+                u = work.tile([P, Q], F32, name="u", bufs=2)
                 for h in (0, 1):
                     s = slice(h * 512, (h + 1) * 512)
                     nc.vector.scalar_tensor_tensor(out=u[:, s], in0=hs[i][:, s], scalar=0.5, in1=bks[i, h][:], op0=ALU.subtract, op1=ALU.mult)
@@ -198,11 +205,16 @@ def tile_incrementalpredictivecodingupdate_kernel(tc, x1, x2, w1_bytes, w1_scale
                 if i in ON_G:
                     nc.gpsimd.tensor_tensor(out=o[:], in0=xh[i][:], in1=us[i][:], op=ALU.subtract)
                 else:
-                    nc.vector.scalar_tensor_tensor(out=o[:], in0=x1s[:, i // 4, i % 4, :], scalar=0.5, in1=us[i][:], op0=ALU.mult, op1=ALU.subtract)
+                    for h in (0, 1):
+                        s = slice(h * 512, (h + 1) * 512)
+                        nc.vector.scalar_tensor_tensor(out=o[:, s], in0=x1s[:, i // 4, i % 4, s], scalar=0.5, in1=us[i][:, s], op0=ALU.mult, op1=ALU.subtract)
+                        nc.sync.dma_start(out=xov[i // 4][:, i % 4, s], in_=o[:, s])
+                    return
                 nc.sync.dma_start(out=xov[i // 4][:, i % 4, :], in_=o[:])
 
             def scale_fa(i):
-                nc.scalar.activation(out=fap[i // 4][:, i % 4, :], in_=f[:, i // 4, i % 4, :], func=ACT.Copy, scale=af[:, i // 4, i % 4:i % 4 + 1])
+                s = slice(512 if i < 4 else 0, Q)
+                nc.scalar.activation(out=fap[i // 4][:, i % 4, s], in_=f[:, i // 4, i % 4, s], func=ACT.Copy, scale=af[:, i // 4, i % 4:i % 4 + 1])
 
             def inter(eng_copy, out, in_):
                 eng_copy(out=out.rearrange("p (c i) t -> p c t i", i=4), in_=in_.rearrange("p t (c i) -> p c t i", i=4))
@@ -214,6 +226,22 @@ def tile_incrementalpredictivecodingupdate_kernel(tc, x1, x2, w1_bytes, w1_scale
                 o = k * Q + h * 512
                 nc.vector.quantize_mx(out=fac[:, o:o + 512].bitcast(FP8X4), scales=fae[:, o:o + 512],
                                       in_=fai[k][:, h * 512:(h + 1) * 512, :].rearrange("p q t -> p (q t)"))
+
+            gaps = []
+
+            def gap_piece(k, b, kind):
+                z = work.tile([P, P, 4], BF16, name="z", bufs=1, align_bytes=64)
+                src, gain, codes, scales, width = (eps, cs, ecc, ece, R) if kind == 0 else (f, as_, fac, fae, Q)
+                s = slice(b * P, (b + 1) * P)
+                nc.gpsimd.tensor_tensor(out=z[:], in0=src[:, k, :, s].rearrange("p t q -> p q t"),
+                                        in1=gain[:, k, :].unsqueeze(1).to_broadcast([P, P, 4]), op=ALU.mult)
+                o = k * width + b * P
+                gaps.append((codes[:, o:o + P], scales[:, o:o + P], z))
+
+            def gap_quant():
+                if gaps:
+                    cd, sc, z = gaps.pop(0)
+                    nc.vector.quantize_mx(out=cd.bitcast(FP8X4), scales=sc, in_=z[:].rearrange("p q t -> p (q t)"))
 
             ecs = {}
 
@@ -238,8 +266,8 @@ def tile_incrementalpredictivecodingupdate_kernel(tc, x1, x2, w1_bytes, w1_scale
                                         rhs=ecc[:, k * R:(k + 1) * R].bitcast(FP8X4), rhs_scale=ece[:, k * R:(k + 1) * R],
                                         start=(k == 0), stop=(k == 1))
                 d = work.tile([P, R], F32, name="d", bufs=8)
-                nc.scalar.activation(out=d[:], in_=dw[:], func=ACT.Copy, scale=0.03125)
-                nc.sync.dma_start(out=out_1[m * P:(m + 1) * P, :], in_=d[:])
+                nc.scalar.activation(out=d[:].rearrange("p (m u) -> p m u", u=4), in_=dw[:].rearrange("p (u m) -> p m u", u=4), func=ACT.Copy, scale=0.03125)
+                nc.sync.dma_start(out=dwv[m // 4, m % 4], in_=d[:])
 
             def widen(k, t):
                 nc.vector.tensor_scalar(out=w1p[:, k, t, :], in0=w1b[:, k, t, :].bitcast(FP8), scalar1=w1s[:, k, t:t + 1], scalar2=None, op0=ALU.mult)
@@ -255,8 +283,6 @@ def tile_incrementalpredictivecodingupdate_kernel(tc, x1, x2, w1_bytes, w1_scale
                 nc.vector.quantize_mx(out=v1c[:, h * 512:(h + 1) * 512].bitcast(FP8X4), scales=v1e[:, h * 512:(h + 1) * 512],
                                       in_=v1i[:, h * 512:(h + 1) * 512, :].rearrange("p q t -> p (q t)"))
 
-            LEAD = 3
-            SIDE = (0, 0, 0, 3, 6, 9, 12, 16)
             for i in range(2):
                 tanh(i)
             for k in (0, 1):
@@ -269,19 +295,21 @@ def tile_incrementalpredictivecodingupdate_kernel(tc, x1, x2, w1_bytes, w1_scale
             inter(nc.vector.tensor_copy, w1i[:, 1, 256:], w1p[:, 1, :, 256:])
             tanh(2)
             tanh(3)
-            inter_v1(0)
-            inter_v1(1)
-            inter_v1(2)
-            inter_v1(3)
+            for q in range(4):
+                inter_v1(q)
             for i in range(4, 8):
                 tanh(i)
-            side = []
-            for k in (0, 1):
-                side += [(scale_fa, 4 * k + t) for t in range(4)] + [(inter_fa, k, h) for h in range(4)]
+            side = [(scale_fa, t) for t in range(4)] + [(inter_fa, 0, 2), (inter_fa, 0, 3)] + [(scale_fa, 4 + t) for t in range(4)] + [(inter_fa, 1, h) for h in range(4)]
             nside = 0
 
             for s in range(8):
-                j = s - 2
+                j = s - 3
+                if s == 1:
+                    z0 = work.tile([P, P, 4], BF16, name="z", bufs=1, align_bytes=64)
+                    nc.vector.memset(z0[:, 0:1, 0:2], 0.0)
+                if s in (1, 2, 3, 4):
+                    gap_quant()
+                    gap_piece(0, s - 1, 1)
                 mul_g(s)
                 if s < 7:
                     trans_f(s + 1)
@@ -300,52 +328,56 @@ def tile_incrementalpredictivecodingupdate_kernel(tc, x1, x2, w1_bytes, w1_scale
                     quant_v1(1)
                 if j >= 0:
                     quant_ep(j)
-                    mm2(j)
                 if j + 1 >= 0:
                     trans_e(j + 1)
-                if s == 4:
-                    mul_c(0, 0)
-                if s == 5:
-                    mul_c(0, 1)
-                if s == 6:
-                    quant_ec(0)
-                    quant_fa(0, 0)
-                if s == 7:
-                    quant_fa(0, 1)
                 if j >= 0:
                     half_x(j + 1)
-                if 0 <= j < 5:
                     square(j)
-                while nside < SIDE[s]:
+                while nside < (0, 0, 0, 3, 6, 9, 11, 14)[s]:
                     side[nside][0](*side[nside][1:])
                     nside += 1
+                if s >= 4:
+                    gap_quant()
+                    gap_piece(0, s - 4, 0)
+                if s == 7:
+                    quant_fa(0, 1)
                 if j >= 1:
                     delta(j - 1)
                     state(j - 1)
-
+                if j >= 0:
+                    mm2(j)
             error(7)
-            mul_p(6)
-            trans_e(7)
-            quant_ep(6)
-            mm2(6)
+            mul_p(5)
+            square(5)
+            delta(4)
+            gap_quant()
+            quant_ep(5)
+            trans_e(6)
             mul_c(1, 0)
-            mul_p(7)
+            state(4)
+            mm2(5)
             mul_c(1, 1)
-            quant_ep(7)
+            mul_p(6)
             quant_fa(1, 0)
             quant_fa(1, 1)
             quant_ec(1)
-            square(5)
+            quant_ep(6)
+            trans_e(7)
             square(6)
-            for m in range(6):
+            square(7)
+            for m in range(3):
                 mm3(m)
             delta(5)
             state(5)
+            mm2(6)
+            mul_p(7)
+            for m in range(3, 6):
+                mm3(m)
+            quant_ep(7)
             delta(6)
+            state(6)
             mm2(7)
-            square(7)
             for m in range(6, 8):
                 mm3(m)
-            state(6)
             delta(7)
             state(7)

@@ -17,6 +17,7 @@ ALU = mybir.AluOpType
 ACT = mybir.ActivationFunctionType
 
 HALF_ROOT = 0.5 ** 0.5
+GC = 704
 ON_G = (0, 1, 2, 3)
 
 
@@ -70,9 +71,9 @@ def tile_incrementalpredictivecodingupdate_kernel(tc, x1, x2, w1_bytes, w1_scale
             nc.scalar.dma_start(out=w1s[:], in_=w1_scale.rearrange("(g p t) o -> p g (t o)", p=P, t=4))
             nc.scalar.dma_start(out=gs[:], in_=g.rearrange("(g p t) -> p g t", p=P, t=4))
             nc.sync.dma_start(out=w1b[:, 0], in_=w1v[0])
-            nc.sync.dma_start(out=x1s[:, 0, 0, :], in_=x1v[0][:, 0, :])
             nc.scalar.dma_start(out=as_[:], in_=a.rearrange("(g p t) -> p g t", p=P, t=4))
             nc.sync.dma_start(out=w1b[:, 1], in_=w1v[1])
+            nc.sync.dma_start(out=x1s[:, 0, 0, :], in_=x1v[0][:, 0, :])
             for t in (1, 2, 3):
                 nc.sync.dma_start(out=x1s[:, 0, t, :], in_=x1v[0][:, t, :])
             nc.sync.dma_start(out=v1s[:, :, 0:512], in_=v1v[:, :, 0:512])
@@ -106,6 +107,11 @@ def tile_incrementalpredictivecodingupdate_kernel(tc, x1, x2, w1_bytes, w1_scale
                     nc.scalar.activation(out=h[:, s].rearrange("p (b j u) -> p b u j", j=4, u=4),
                                          in_=f[:, i // 4, i % 4, s].rearrange("p (u b j) -> p b u j", u=4, j=4), func=ACT.Square, scale=HALF_ROOT)
                 hs[i] = h
+
+            def warm_up(n):
+                for e in range(n):
+                    idle = psum.tile([P, 512], F32, name="idle", tag="ft", bufs=4)
+                    nc.tensor.matmul(idle[:], lhsT=ecs[1][:, 256:288, :].rearrange("p r t -> p (r t)"), rhs=ecs[1][:, 256:384, :].rearrange("p r t -> p (r t)"), start=True, stop=True)
 
             fts = {}
 
@@ -190,7 +196,7 @@ def tile_incrementalpredictivecodingupdate_kernel(tc, x1, x2, w1_bytes, w1_scale
             def half_x(i):
                 if i in ON_G:
                     y = work.tile([P, Q], BF16, name="y", bufs=3)
-                    nc.vector.tensor_scalar(out=y[:], in0=x1s[:, i // 4, i % 4, :], scalar1=0.5, scalar2=None, op0=ALU.mult)
+                    nc.vector.tensor_scalar(out=y[:, :GC], in0=x1s[:, i // 4, i % 4, :GC], scalar1=0.5, scalar2=None, op0=ALU.mult)
                     xh[i] = y
 
             def delta(i):
@@ -200,10 +206,20 @@ def tile_incrementalpredictivecodingupdate_kernel(tc, x1, x2, w1_bytes, w1_scale
                     nc.vector.scalar_tensor_tensor(out=u[:, s], in0=hs[i][:, s], scalar=0.5, in1=bks[i, h][:], op0=ALU.subtract, op1=ALU.mult)
                 us[i] = u
 
+            outs = {}
+
+            def state_rest(i):
+                o = outs[i]
+                if GC < Q:
+                    nc.vector.scalar_tensor_tensor(out=o[:, GC:], in0=x1s[:, i // 4, i % 4, GC:], scalar=0.5, in1=us[i][:, GC:], op0=ALU.mult, op1=ALU.subtract)
+                nc.sync.dma_start(out=xov[i // 4][:, i % 4, :], in_=o[:])
+
             def state(i):
                 o = work.tile([P, Q], F32, name="o", bufs=3)
                 if i in ON_G:
-                    nc.gpsimd.tensor_tensor(out=o[:], in0=xh[i][:], in1=us[i][:], op=ALU.subtract)
+                    nc.gpsimd.tensor_tensor(out=o[:, :GC], in0=xh[i][:, :GC], in1=us[i][:, :GC], op=ALU.subtract)
+                    outs[i] = o
+                    return
                 else:
                     for h in (0, 1):
                         s = slice(h * 512, (h + 1) * 512)
@@ -269,6 +285,9 @@ def tile_incrementalpredictivecodingupdate_kernel(tc, x1, x2, w1_bytes, w1_scale
                 nc.scalar.activation(out=d[:].rearrange("p (m u) -> p m u", u=4), in_=dw[:].rearrange("p (u m) -> p m u", u=4), func=ACT.Copy, scale=0.03125)
                 nc.sync.dma_start(out=dwv[m // 4, m % 4], in_=d[:])
 
+            def widen_s(k, t):
+                nc.scalar.activation(out=w1p[:, k, t, :], in_=w1b[:, k, t, :].bitcast(FP8), func=ACT.Copy, scale=w1s[:, k, t:t + 1])
+
             def widen(k, t):
                 nc.vector.tensor_scalar(out=w1p[:, k, t, :], in0=w1b[:, k, t, :].bitcast(FP8), scalar1=w1s[:, k, t:t + 1], scalar2=None, op0=ALU.mult)
 
@@ -283,11 +302,14 @@ def tile_incrementalpredictivecodingupdate_kernel(tc, x1, x2, w1_bytes, w1_scale
                 nc.vector.quantize_mx(out=v1c[:, h * 512:(h + 1) * 512].bitcast(FP8X4), scales=v1e[:, h * 512:(h + 1) * 512],
                                       in_=v1i[:, h * 512:(h + 1) * 512, :].rearrange("p q t -> p (q t)"))
 
+            widen_s(0, 0)
+            widen_s(0, 1)
             for i in range(2):
                 tanh(i)
             for k in (0, 1):
                 for t in range(4):
-                    widen(k, t)
+                    if (k, t) not in ((0, 0), (0, 1)):
+                        widen(k, t)
             trans_f(0)
             inter(nc.vector.tensor_copy, w1i[:, 0], w1p[:, 0])
             inter(nc.scalar.copy, w1i[:, 1, :256], w1p[:, 1, :, :256])
@@ -323,11 +345,13 @@ def tile_incrementalpredictivecodingupdate_kernel(tc, x1, x2, w1_bytes, w1_scale
                     half_x(0)
                 quant_fg(s)
                 mm1(s)
-                if s == 2:
+                if s == 3:
                     quant_v1(0)
                     quant_v1(1)
                 if j >= 0:
                     quant_ep(j)
+                if j >= 2:
+                    state_rest(j - 2)
                 if j + 1 >= 0:
                     trans_e(j + 1)
                 if j >= 0:
@@ -339,8 +363,6 @@ def tile_incrementalpredictivecodingupdate_kernel(tc, x1, x2, w1_bytes, w1_scale
                 if s >= 4:
                     gap_quant()
                     gap_piece(0, s - 4, 0)
-                if s == 7:
-                    quant_fa(0, 1)
                 if j >= 1:
                     delta(j - 1)
                     state(j - 1)
@@ -352,31 +374,36 @@ def tile_incrementalpredictivecodingupdate_kernel(tc, x1, x2, w1_bytes, w1_scale
             delta(4)
             gap_quant()
             quant_ep(5)
+            state_rest(3)
             trans_e(6)
-            mul_c(1, 0)
-            state(4)
             mm2(5)
+            mul_c(1, 0)
             mul_c(1, 1)
-            mul_p(6)
+            warm_up(4)
+            quant_fa(0, 1)
             quant_fa(1, 0)
             quant_fa(1, 1)
             quant_ec(1)
-            quant_ep(6)
-            trans_e(7)
             square(6)
             square(7)
-            for m in range(3):
+            mul_p(6)
+            state(4)
+            for m in range(2):
                 mm3(m)
+            trans_e(7)
+            for m in range(2, 4):
+                mm3(m)
+            quant_ep(6)
             delta(5)
-            state(5)
             mm2(6)
             mul_p(7)
-            for m in range(3, 6):
+            state(5)
+            for m in range(4, 6):
                 mm3(m)
             quant_ep(7)
             delta(6)
-            state(6)
             mm2(7)
+            state(6)
             for m in range(6, 8):
                 mm3(m)
             delta(7)

from contextlib import ExitStack

import concourse.mybir as mybir
from concourse.masks import make_identity

N, Q, R = 1024, 1024, 512
P = 128
FLOPS = 3 * 2 * N * Q * R

F32 = mybir.dt.float32
BF16 = mybir.dt.bfloat16
U32 = mybir.dt.uint32
U8 = mybir.dt.uint8
FP8 = mybir.dt.float8_e4m3fn
FP8X4 = mybir.dt.float8_e4m3fn_x4
ALU = mybir.AluOpType
ACT = mybir.ActivationFunctionType

HALF_ROOT = 0.5 ** 0.5
GC = 704
ON_G = (0, 1, 2, 3)


def tile_incrementalpredictivecodingupdate_kernel(tc, x1, x2, w1_bytes, w1_scale, v1, g, pi2, a, c, out_0, out_1):
    nc = tc.nc
    x1v = x1.rearrange("(g p t) q -> g p t q", p=P, t=4)
    x2v = x2.rearrange("(g p t) r -> g p t r", p=P, t=4)
    w1v = w1_bytes.rearrange("(g p t) r -> g p t r", p=P, t=4)
    v1v = v1.rearrange("(p t) q -> p t q", t=4)
    dwv = out_1.rearrange("(k p u) r -> k u p r", k=2, u=4)
    xov = out_0.rearrange("(g p t) q -> g p t q", p=P, t=4)

    with ExitStack() as ctx:
        keep = ctx.enter_context(tc.tile_pool(name="keep", bufs=1))
        work = ctx.enter_context(tc.tile_pool(name="work", bufs=2))
        psum = ctx.enter_context(tc.psum_pool(name="psum", bufs=1))

        x1s = keep.tile([P, 2, 4, Q], BF16, name="x1s")
        x2s = keep.tile([P, 2, 4, R], BF16, name="x2s")
        w1b = keep.tile([P, 2, 4, R], U8, name="w1b")
        w1s = keep.tile([P, 2, 4], F32, name="w1s")
        v1s = keep.tile([P, 4, Q], BF16, name="v1s")
        gs = keep.tile([P, 2, 4], BF16, name="gs")
        as_ = keep.tile([P, 2, 4], BF16, name="as_")
        cs = keep.tile([P, 2, 4], BF16, name="cs")
        ps = keep.tile([P, 4], BF16, name="ps")
        ident = keep.tile([P, P], F32, name="ident")

        f = keep.tile([P, 2, 4, Q], F32, name="f")
        eps = keep.tile([P, 2, 4, R], F32, name="eps")
        w1p = keep.tile([P, 2, 4, R], BF16, name="w1p")
        w1i = keep.tile([P, 2, R, 4], BF16, name="w1i", tag="inter", bufs=3, align_bytes=64)
        v1i = keep.tile([P, Q, 4], BF16, name="v1i", tag="inter", bufs=3, align_bytes=64)
        fai = []
        fap = []
        for k in (0, 1):
            fai_k = keep.tile([P, Q, 4], BF16, name="fai%d" % k, tag="inter", bufs=3, align_bytes=64)
            fai.append(fai_k)
            fap_k = keep.tile([P, 4, Q], BF16, name="fap%d" % k)
            fap.append(fap_k)
        w1c = keep.tile([P, 2 * R], U32, name="w1c", align_bytes=64)
        w1e = keep.tile([P, 2 * R], U8, name="w1e", align_bytes=64)
        v1c = keep.tile([P, Q], U32, name="v1c", align_bytes=64)
        v1e = keep.tile([P, Q], U8, name="v1e", align_bytes=64)
        fac = keep.tile([P, 2 * Q], U32, name="fac", align_bytes=64)
        fae = keep.tile([P, 2 * Q], U8, name="fae", align_bytes=64)
        ecc = keep.tile([P, 2 * R], U32, name="ecc", align_bytes=64)
        ece = keep.tile([P, 2 * R], U8, name="ece", align_bytes=64)

        with tc.manual_schedule():
            nc.scalar.dma_start(out=w1s[:], in_=w1_scale.rearrange("(g p t) o -> p g (t o)", p=P, t=4))
            nc.scalar.dma_start(out=gs[:], in_=g.rearrange("(g p t) -> p g t", p=P, t=4))
            nc.sync.dma_start(out=w1b[:, 0], in_=w1v[0])
            nc.scalar.dma_start(out=as_[:], in_=a.rearrange("(g p t) -> p g t", p=P, t=4))
            nc.sync.dma_start(out=w1b[:, 1], in_=w1v[1])
            nc.sync.dma_start(out=x1s[:, 0, 0, :], in_=x1v[0][:, 0, :])
            for t in (1, 2, 3):
                nc.sync.dma_start(out=x1s[:, 0, t, :], in_=x1v[0][:, t, :])
            nc.sync.dma_start(out=v1s[:, :, 0:512], in_=v1v[:, :, 0:512])
            nc.sync.dma_start(out=x2s[:, 0], in_=x2v[0])
            nc.sync.dma_start(out=v1s[:, :, 512:1024], in_=v1v[:, :, 512:1024])
            for t in (0, 2):
                nc.sync.dma_start(out=x1s[:, 1, t:t + 2, :], in_=x1v[1][:, t:t + 2, :])
            nc.sync.dma_start(out=x2s[:, 1], in_=x2v[1])
            make_identity(nc, ident[:])
            nc.gpsimd.dma_start(out=ps[:], in_=pi2.rearrange("(p t) -> p t", t=4))
            nc.gpsimd.dma_start(out=cs[:], in_=c.rearrange("(g p t) -> p g t", p=P, t=4))

            warm = keep.tile([P, 1], F32, name="warm")
            warm2 = keep.tile([P, 1], F32, name="warm2")
            nc.vector.memset(warm[:], 0.0)
            nc.scalar.activation(out=warm2[:], in_=warm[:], func=ACT.Tanh)

            af = keep.tile([P, 2, 4], F32, name="af")
            nc.gpsimd.tensor_copy(out=af[:], in_=as_[:])

            def tanh(i):
                nc.scalar.activation(out=f[:, i // 4, i % 4, :].rearrange("p (k u m) -> p k u m", k=2, u=4),
                                     in_=x1s[:, i // 4, i % 4, :].rearrange("p (k m u) -> p k u m", k=2, u=4), func=ACT.Tanh)

            hs = {}

            def square(i):
                h = work.tile([P, Q], F32, name="h", bufs=3)
                for k in (0, 1):
                    s = slice(k * 512, (k + 1) * 512)
                    nc.scalar.activation(out=h[:, s].rearrange("p (b j u) -> p b u j", j=4, u=4),
                                         in_=f[:, i // 4, i % 4, s].rearrange("p (u b j) -> p b u j", u=4, j=4), func=ACT.Square, scale=HALF_ROOT)
                hs[i] = h

            def warm_up(n):
                for e in range(n):
                    idle = psum.tile([P, 512], F32, name="idle", tag="ft", bufs=4)
                    nc.tensor.matmul(idle[:], lhsT=ecs[1][:, 256:288, :].rearrange("p r t -> p (r t)"), rhs=ecs[1][:, 256:384, :].rearrange("p r t -> p (r t)"), start=True, stop=True)

            fts = {}

            def trans_f(i):
                for k in (0, 1):
                    ft = psum.tile([P, 4, P], F32, name="ft", tag="ft", bufs=4)
                    for t in range(4):
                        nc.tensor.transpose(ft[:, t, :], f[:, i // 4, i % 4, k * 512 + t * P:k * 512 + (t + 1) * P], ident[:])
                    fts[i, k] = ft

            fgs = {}

            def mul_g(i):
                fg = work.tile([P, 2, P, 4], BF16, name="fg", align_bytes=64)
                for k in (0, 1):
                    nc.vector.tensor_tensor(out=fg[:, k], in0=fts[i, k][:].rearrange("p t n -> p n t"),
                                            in1=gs[:, k, :].unsqueeze(1).to_broadcast([P, P, 4]), op=ALU.mult)
                fgs[i] = fg

            fgq = {}

            def quant_fg(i):
                cd = work.tile([P, 2 * P], U32, name="fgc", align_bytes=64)
                sc = work.tile([P, 2 * P], U8, name="fge", align_bytes=64)
                nc.vector.quantize_mx(out=cd[:].bitcast(FP8X4), scales=sc[:], in_=fgs[i][:].rearrange("p k n t -> p (k n t)"))
                fgq[i] = (cd, sc)

            mus = {}

            def mm1(i):
                mu = psum.tile([P, R], F32, name="mu", tag="mu")
                cd, sc = fgq[i]
                for k in (0, 1):
                    nc.tensor.matmul_mx(out=mu[:], lhsT=cd[:, k * P:(k + 1) * P].bitcast(FP8X4), lhsT_scale=sc[:, k * P:(k + 1) * P],
                                        rhs=w1c[:, k * R:(k + 1) * R].bitcast(FP8X4), rhs_scale=w1e[:, k * R:(k + 1) * R],
                                        start=(k == 0), stop=(k == 1))
                mus[i] = mu

            def error(i):
                nc.vector.tensor_tensor(out=eps[:, i // 4, i % 4, :].rearrange("p (u m) -> p u m", u=4),
                                        in0=x2s[:, i // 4, i % 4, :].rearrange("p (m u) -> p u m", u=4),
                                        in1=mus[i][:].rearrange("p (m u) -> p u m", u=4), op=ALU.subtract)

            ets = {}

            def trans_e(i):
                et = psum.tile([P, 4, P], F32, name="et", tag="et")
                for t in range(4):
                    nc.tensor.transpose(et[:, t, :], eps[:, i // 4, i % 4, t * P:(t + 1) * P], ident[:])
                ets[i] = et

            eps_ = {}

            def mul_p(i):
                ep = work.tile([P, P, 4], BF16, name="ep", align_bytes=64)
                nc.vector.tensor_tensor(out=ep[:], in0=ets[i][:].rearrange("p t n -> p n t"),
                                        in1=ps[:].unsqueeze(1).to_broadcast([P, P, 4]), op=ALU.mult)
                eps_[i] = ep

            epq = {}

            def quant_ep(i):
                cd = work.tile([P, P], U32, name="epc", align_bytes=64)
                sc = work.tile([P, P], U8, name="epe", align_bytes=64)
                nc.vector.quantize_mx(out=cd[:].bitcast(FP8X4), scales=sc[:], in_=eps_[i][:].rearrange("p n t -> p (n t)"))
                epq[i] = (cd, sc)

            bks = {}

            def mm2(i):
                cd, sc = epq[i]
                for h in (0, 1):
                    bk = psum.tile([P, 512], F32, name="bk", tag="bk", bufs=2)
                    nc.tensor.matmul_mx(out=bk[:], lhsT=cd[:].bitcast(FP8X4), lhsT_scale=sc[:],
                                        rhs=v1c[:, h * 512:(h + 1) * 512].bitcast(FP8X4), rhs_scale=v1e[:, h * 512:(h + 1) * 512],
                                        start=True, stop=True)
                    bks[i, h] = bk

            us = {}
            xh = {}

            def half_x(i):
                if i in ON_G:
                    y = work.tile([P, Q], BF16, name="y", bufs=3)
                    nc.vector.tensor_scalar(out=y[:, :GC], in0=x1s[:, i // 4, i % 4, :GC], scalar1=0.5, scalar2=None, op0=ALU.mult)
                    xh[i] = y

            def delta(i):
                u = work.tile([P, Q], F32, name="u", bufs=2)
                for h in (0, 1):
                    s = slice(h * 512, (h + 1) * 512)
                    nc.vector.scalar_tensor_tensor(out=u[:, s], in0=hs[i][:, s], scalar=0.5, in1=bks[i, h][:], op0=ALU.subtract, op1=ALU.mult)
                us[i] = u

            outs = {}

            def state_rest(i):
                o = outs[i]
                if GC < Q:
                    nc.vector.scalar_tensor_tensor(out=o[:, GC:], in0=x1s[:, i // 4, i % 4, GC:], scalar=0.5, in1=us[i][:, GC:], op0=ALU.mult, op1=ALU.subtract)
                nc.sync.dma_start(out=xov[i // 4][:, i % 4, :], in_=o[:])

            def state(i):
                o = work.tile([P, Q], F32, name="o", bufs=3)
                if i in ON_G:
                    nc.gpsimd.tensor_tensor(out=o[:, :GC], in0=xh[i][:, :GC], in1=us[i][:, :GC], op=ALU.subtract)
                    outs[i] = o
                    return
                else:
                    for h in (0, 1):
                        s = slice(h * 512, (h + 1) * 512)
                        nc.vector.scalar_tensor_tensor(out=o[:, s], in0=x1s[:, i // 4, i % 4, s], scalar=0.5, in1=us[i][:, s], op0=ALU.mult, op1=ALU.subtract)
                        nc.sync.dma_start(out=xov[i // 4][:, i % 4, s], in_=o[:, s])
                    return
                nc.sync.dma_start(out=xov[i // 4][:, i % 4, :], in_=o[:])

            def scale_fa(i):
                s = slice(512 if i < 4 else 0, Q)
                nc.scalar.activation(out=fap[i // 4][:, i % 4, s], in_=f[:, i // 4, i % 4, s], func=ACT.Copy, scale=af[:, i // 4, i % 4:i % 4 + 1])

            def inter(eng_copy, out, in_):
                eng_copy(out=out.rearrange("p (c i) t -> p c t i", i=4), in_=in_.rearrange("p t (c i) -> p c t i", i=4))

            def inter_fa(k, h):
                inter(nc.scalar.copy, fai[k][:, h * 256:(h + 1) * 256, :], fap[k][:, :, h * 256:(h + 1) * 256])

            def quant_fa(k, h):
                o = k * Q + h * 512
                nc.vector.quantize_mx(out=fac[:, o:o + 512].bitcast(FP8X4), scales=fae[:, o:o + 512],
                                      in_=fai[k][:, h * 512:(h + 1) * 512, :].rearrange("p q t -> p (q t)"))

            gaps = []

            def gap_piece(k, b, kind):
                z = work.tile([P, P, 4], BF16, name="z", bufs=1, align_bytes=64)
                src, gain, codes, scales, width = (eps, cs, ecc, ece, R) if kind == 0 else (f, as_, fac, fae, Q)
                s = slice(b * P, (b + 1) * P)
                nc.gpsimd.tensor_tensor(out=z[:], in0=src[:, k, :, s].rearrange("p t q -> p q t"),
                                        in1=gain[:, k, :].unsqueeze(1).to_broadcast([P, P, 4]), op=ALU.mult)
                o = k * width + b * P
                gaps.append((codes[:, o:o + P], scales[:, o:o + P], z))

            def gap_quant():
                if gaps:
                    cd, sc, z = gaps.pop(0)
                    nc.vector.quantize_mx(out=cd.bitcast(FP8X4), scales=sc, in_=z[:].rearrange("p q t -> p (q t)"))

            ecs = {}

            def mul_c(k, h):
                if h == 0:
                    ec = work.tile([P, R, 4], BF16, name="ec", align_bytes=64)
                    ecs[k] = ec
                s = slice(h * 256, (h + 1) * 256)
                nc.vector.tensor_tensor(out=ecs[k][:, s, :].rearrange("p (c i) t -> p c t i", i=4),
                                        in0=eps[:, k, :, s].rearrange("p t (c i) -> p c t i", i=4),
                                        in1=cs[:, k, :].unsqueeze(1).unsqueeze(3).to_broadcast([P, 64, 4, 4]), op=ALU.mult)

            def quant_ec(k):
                nc.vector.quantize_mx(out=ecc[:, k * R:(k + 1) * R].bitcast(FP8X4), scales=ece[:, k * R:(k + 1) * R],
                                      in_=ecs[k][:].rearrange("p r t -> p (r t)"))

            def mm3(m):
                dw = psum.tile([P, R], F32, name="dw", tag="ft", bufs=4)
                for k in (0, 1):
                    o = k * Q + m * P
                    nc.tensor.matmul_mx(out=dw[:], lhsT=fac[:, o:o + P].bitcast(FP8X4), lhsT_scale=fae[:, o:o + P],
                                        rhs=ecc[:, k * R:(k + 1) * R].bitcast(FP8X4), rhs_scale=ece[:, k * R:(k + 1) * R],
                                        start=(k == 0), stop=(k == 1))
                d = work.tile([P, R], F32, name="d", bufs=8)
                nc.scalar.activation(out=d[:].rearrange("p (m u) -> p m u", u=4), in_=dw[:].rearrange("p (u m) -> p m u", u=4), func=ACT.Copy, scale=0.03125)
                nc.sync.dma_start(out=dwv[m // 4, m % 4], in_=d[:])

            def widen_s(k, t):
                nc.scalar.activation(out=w1p[:, k, t, :], in_=w1b[:, k, t, :].bitcast(FP8), func=ACT.Copy, scale=w1s[:, k, t:t + 1])

            def widen(k, t):
                nc.vector.tensor_scalar(out=w1p[:, k, t, :], in0=w1b[:, k, t, :].bitcast(FP8), scalar1=w1s[:, k, t:t + 1], scalar2=None, op0=ALU.mult)

            def quant_w1(k):
                nc.vector.quantize_mx(out=w1c[:, k * R:(k + 1) * R].bitcast(FP8X4), scales=w1e[:, k * R:(k + 1) * R],
                                      in_=w1i[:, k].rearrange("p r t -> p (r t)"))

            def inter_v1(h):
                inter(nc.scalar.copy, v1i[:, h * 256:(h + 1) * 256, :], v1s[:, :, h * 256:(h + 1) * 256])

            def quant_v1(h):
                nc.vector.quantize_mx(out=v1c[:, h * 512:(h + 1) * 512].bitcast(FP8X4), scales=v1e[:, h * 512:(h + 1) * 512],
                                      in_=v1i[:, h * 512:(h + 1) * 512, :].rearrange("p q t -> p (q t)"))

            widen_s(0, 0)
            widen_s(0, 1)
            for i in range(2):
                tanh(i)
            for k in (0, 1):
                for t in range(4):
                    if (k, t) not in ((0, 0), (0, 1)):
                        widen(k, t)
            trans_f(0)
            inter(nc.vector.tensor_copy, w1i[:, 0], w1p[:, 0])
            inter(nc.scalar.copy, w1i[:, 1, :256], w1p[:, 1, :, :256])
            quant_w1(0)
            inter(nc.vector.tensor_copy, w1i[:, 1, 256:], w1p[:, 1, :, 256:])
            tanh(2)
            tanh(3)
            for q in range(4):
                inter_v1(q)
            for i in range(4, 8):
                tanh(i)
            side = [(scale_fa, t) for t in range(4)] + [(inter_fa, 0, 2), (inter_fa, 0, 3)] + [(scale_fa, 4 + t) for t in range(4)] + [(inter_fa, 1, h) for h in range(4)]
            nside = 0

            for s in range(8):
                j = s - 3
                if s == 1:
                    z0 = work.tile([P, P, 4], BF16, name="z", bufs=1, align_bytes=64)
                    nc.vector.memset(z0[:, 0:1, 0:2], 0.0)
                if s in (1, 2, 3, 4):
                    gap_quant()
                    gap_piece(0, s - 1, 1)
                mul_g(s)
                if s < 7:
                    trans_f(s + 1)
                if s == 0:
                    quant_w1(1)
                if s >= 1:
                    error(s - 1)
                if j >= 0:
                    mul_p(j)
                if s == 2:
                    half_x(0)
                quant_fg(s)
                mm1(s)
                if s == 3:
                    quant_v1(0)
                    quant_v1(1)
                if j >= 0:
                    quant_ep(j)
                if j >= 2:
                    state_rest(j - 2)
                if j + 1 >= 0:
                    trans_e(j + 1)
                if j >= 0:
                    half_x(j + 1)
                    square(j)
                while nside < (0, 0, 0, 3, 6, 9, 11, 14)[s]:
                    side[nside][0](*side[nside][1:])
                    nside += 1
                if s >= 4:
                    gap_quant()
                    gap_piece(0, s - 4, 0)
                if j >= 1:
                    delta(j - 1)
                    state(j - 1)
                if j >= 0:
                    mm2(j)
            error(7)
            mul_p(5)
            square(5)
            delta(4)
            gap_quant()
            quant_ep(5)
            state_rest(3)
            trans_e(6)
            mm2(5)
            mul_c(1, 0)
            mul_c(1, 1)
            warm_up(4)
            quant_fa(0, 1)
            quant_fa(1, 0)
            quant_fa(1, 1)
            quant_ec(1)
            square(6)
            square(7)
            mul_p(6)
            state(4)
            for m in range(2):
                mm3(m)
            trans_e(7)
            for m in range(2, 4):
                mm3(m)
            quant_ep(6)
            delta(5)
            mm2(6)
            mul_p(7)
            state(5)
            for m in range(4, 6):
                mm3(m)
            quant_ep(7)
            delta(6)
            mm2(7)
            state(6)
            for m in range(6, 8):
                mm3(m)
            delta(7)
            state(7)
